import numpy as np
import ml_dtypes


def mxq(x, axis, fmt="e4m3"):
    dtype, down = {"e4m3": (ml_dtypes.float8_e4m3fn, 7), "e5m2": (ml_dtypes.float8_e5m2, 14)}[fmt]
    v = np.moveaxis(np.asarray(x, np.float32).astype(ml_dtypes.bfloat16).astype(np.float64), axis, -1)
    blocks = v.reshape(v.shape[:-1] + (-1, 32))
    amax = np.abs(blocks).max(-1, keepdims=True)
    byte = np.maximum(np.where(amax > 0, np.frexp(amax)[1] - 1 + 127, 0) - down, 1)
    scale = np.exp2(byte - 127.0)
    codes = (blocks / scale).astype(np.float32).astype(dtype).astype(np.float64)
    return np.moveaxis((codes * scale).reshape(v.shape), -1, axis)


WIDE = False


def mx_kscale(k):
    if not WIDE:
        return np.ones(k)
    levels = np.array([10, -10, 5, -5, 0])
    if k % 512:
        return np.exp2(np.random.permutation(np.resize(levels, k // 32))).repeat(32)
    a = np.empty((k // 512, 16))
    for p in range(k // 512):
        a[p, :8] = np.random.permutation(np.resize(levels, 8))
        for g in range(8):
            far = levels[np.abs(levels - a[p, g]) >= 10]
            a[p, g + 8] = far[np.random.randint(len(far))]
    return np.exp2(a.ravel()).repeat(32)


def f64(x):
    return np.asarray(x).astype(np.float64)


def striped(idx):
    return np.tile(np.asarray(idx).reshape(-1, 16).T, (8, 1)).astype(np.uint16)


def unstriped(offs):
    return offs[:16].T.reshape(-1).astype(np.int64)


def striped8(idx):
    return np.asarray(idx).reshape(8, -1, 16).transpose(0, 2, 1).reshape(128, -1).astype(np.uint16)


def unstriped8(offs):
    return offs.reshape(8, 16, -1).transpose(0, 2, 1).reshape(8, -1).astype(np.int64)


def pick8(x, idx, run):
    r = np.arange(len(x))
    return x[r[:, None], idx[r % (8 * run) // run]]


E2M1 = np.array([0.0, 0.5, 1.0, 1.5, 2.0, 3.0, 4.0, 6.0, -0.0, -0.5, -1.0, -1.5, -2.0, -3.0, -4.0, -6.0])


def pack_weight(w, fmt):
    k, n = w.shape
    w = f64(np.asarray(w, np.float32).astype(ml_dtypes.bfloat16)).reshape(k // 32, 32, n)
    amax = np.abs(w).max(1)
    if fmt == "e4m3":
        byte = np.frexp(amax)[1] - 1 + 127 - 7
    else:
        mant, ex = np.frexp(amax / 6.0)
        byte = np.where(mant > 0.5, ex, ex - 1) + 127
    byte = np.clip(np.where(amax > 0, byte, 1), 1, 254)
    scaled = (w * np.exp2(127.0 - byte)[:, None, :]).reshape(k, n).astype(np.float32)
    by_word = np.ascontiguousarray(scaled.reshape(k // 512, 128, 4, n).transpose(0, 1, 3, 2))
    if fmt == "e4m3":
        words = by_word.astype(ml_dtypes.float8_e4m3fn).view(np.uint8)
    else:
        c = by_word.astype(ml_dtypes.float4_e2m1fn).view(np.uint8) & 0xF
        words = (c[..., 0::2] | (c[..., 1::2] << 4)).reshape(k // 512, 128, 2 * n)
    return np.ascontiguousarray(words), np.ascontiguousarray(byte.astype(np.uint8).reshape(k // 512, 16, n))


def unpack_weight(words, scales, fmt):
    g, _, n = scales.shape
    words = np.ascontiguousarray(words).reshape(g, 128, n, -1)
    if fmt == "e4m3":
        vals = words.view(ml_dtypes.float8_e4m3fn).astype(np.float64)
    else:
        nib = np.empty((g, 128, n, 4), np.uint8)
        nib[..., 0::2] = words & 0xF
        nib[..., 1::2] = words >> 4
        vals = E2M1[nib]
    vals = vals * np.repeat(np.exp2(scales.astype(np.float64) - 127.0), 8, axis=1)[..., None]
    return vals.transpose(0, 1, 3, 2).reshape(g * 512, n)


K, J, R, T, Z, M, C, O, N, S = 512, 256, 512, 1024, 512, 1024, 512, 256, 256, 1024


def setup_inputs():
    n = np.random.standard_normal
    idx = np.random.permutation(T)[:J]
    idx2 = np.random.permutation(M)[:J]
    idx3 = np.stack([np.random.permutation(C)[:J] for _ in range(8)])
    idx4 = np.stack([np.random.permutation(C)[:J] for _ in range(8)])
    idx5 = np.stack([np.random.permutation(C)[:O] for _ in range(8)])
    idx6 = np.random.permutation(S)[:N]
    fk = mx_kscale(K)
    fr = mx_kscale(R)
    fz = mx_kscale(Z)
    xtp = pack_weight(n((K, T)) * fk[:, None], "e4m3")
    wp = pack_weight(n((K, R)) * 1 / np.sqrt(K) / fk[:, None] * fr, "e2m1")
    xop = pack_weight(n((Z, M)) / fz[:, None], "e2m1")
    w2p = pack_weight(n((Z, R)) * 1 / np.sqrt(Z) * fz[:, None] * fr, "e4m3")
    vsp = pack_weight(n((R, S)) * 1 / np.sqrt(R) / fr[:, None], "e4m3")
    return {
        "xt_words": xtp[0],
        "xt_scales": xtp[1],
        "w_words": wp[0],
        "w_scales": wp[1],
        "xo_words": xop[0],
        "xo_scales": xop[1],
        "w2_words": w2p[0],
        "w2_scales": w2p[1],
        "sa": (np.random.uniform(0.5, 1.6, (R, 1))).astype(np.float32),
        "vs_words": vsp[0],
        "vs_scales": vsp[1],
        "offs": striped(idx),
        "offs2": striped(idx2),
        "offs3": striped8(idx3),
        "offs4": striped8(idx4),
        "offs5": striped8(idx5),
        "offs6": striped(idx6),
    }


def reference(xt_words, xt_scales, w_words, w_scales, xo_words, xo_scales, w2_words, w2_scales, sa, vs_words, vs_scales, offs, offs2, offs3, offs4, offs5, offs6):
    idx = unstriped(offs)
    idx2 = unstriped(offs2)
    idx3 = unstriped8(offs3)
    idx4 = unstriped8(offs4)
    idx5 = unstriped8(offs5)
    idx6 = unstriped(offs6)
    xtu = unpack_weight(xt_words, xt_scales, "e4m3")
    wu = unpack_weight(w_words, w_scales, "e2m1")
    xou = unpack_weight(xo_words, xo_scales, "e2m1")
    w2u = unpack_weight(w2_words, w2_scales, "e4m3")
    vsu = unpack_weight(vs_words, vs_scales, "e4m3")
    xtidxg = xtu[:, idx]
    a = wu.T @ xtidxg
    xoidx2g = xou[:, idx2]
    b = w2u.T @ xoidx2g
    pw = np.zeros((R, C))
    pw[np.arange(R)[:, None], idx3[np.arange(R) % 512 // 64]] = a
    pv = np.zeros((R, C))
    pv[np.arange(R)[:, None], idx4[np.arange(R) % 512 // 64]] = b
    g1 = np.pad(pv, ((0, 0), (1, 0)))[:, :C]
    pg = pw - g1
    hid = pick8(pg, idx5, 64) * f64(sa)
    vsidx6g = vsu[:, idx6]
    hidq = mxq(hid, 0, "e4m3")
    y = vsidx6g.T @ hidq
    return y

@@ -1,0 +1,235 @@
+from contextlib import ExitStack
+
+import concourse.mybir as mybir
+
+K, J, R, T, Z, M, C, O, N, S = 512, 256, 512, 1024, 512, 1024, 512, 256, 256, 1024
+FLOPS = 2 * K * R * J + 2 * Z * R * J + 2 * R * N * O
+
+F32 = mybir.dt.float32
+BF16 = mybir.dt.bfloat16
+I32 = mybir.dt.int32
+U32 = mybir.dt.uint32
+U16 = mybir.dt.uint16
+U8 = mybir.dt.uint8
+FP8X4 = mybir.dt.float8_e4m3fn_x4
+FP4X4 = mybir.dt.float4_e2m1fn_x4
+COPY = mybir.ActivationFunctionType.Copy
+SUB = mybir.AluOpType.subtract
+
+P = 128
+PACK = 4
+QUADS = 4
+HALF = 128
+ALIGN = 64
+
+
+def tile_picked_tokens_plain_two_lagged_store_plain_kernel(
+    tc, xt_words, xt_scales, w_words, w_scales, xo_words, xo_scales, w2_words, w2_scales, sa,
+    vs_words, vs_scales, offs, offs2, offs3, offs4, offs5, offs6, out,
+):
+    nc = tc.nc
+    with ExitStack() as ctx:
+        lists = ctx.enter_context(tc.tile_pool(name="lists", bufs=1))
+        sb = ctx.enter_context(tc.tile_pool(name="sb", bufs=1))
+        psum = ctx.enter_context(tc.psum_pool(name="psum", bufs=8))
+
+        def tile(name, shape, dtype, tag=None):
+            return sb.tile(shape, dtype, name=name, tag=tag or name, align_bytes=ALIGN)
+
+        def load_list(name, src):
+            t = lists.tile([P, J // 16], U16, name=name)
+            nc.sync.dma_start(t[:], src)
+            return t
+
+        def load_words(dst, src):
+            nc.sync.dma_start(out=dst[:].bitcast(I32), in_=src.bitcast(I32))
+
+        def zeroed_plane(name, width, tag=None):
+            t = tile(name, [P, width], U8, tag)
+            nc.vector.memset(t[:].bitcast(I32), 0)
+            return t
+
+        def load_scale_rows(plane, scales, queue=None):
+            for q in range(QUADS):
+                (queue or nc.sync).dma_start(
+                    out=plane[32 * q : 32 * q + 4, :].bitcast(I32),
+                    in_=scales[0][4 * q : 4 * q + 4, :].bitcast(I32),
+                )
+
+        def gather(dst, window, offsets, lo, hi):
+            nc.vector.tensor_copy(out=dst[:, lo:hi], in_=window[:].indirect(offsets[:, lo // 16 : hi // 16]))
+
+        def zeroed_board(name, tag=None):
+            t = tile(name, [P, C], F32, tag)
+            nc.vector.memset(t[:], 0.0)
+            return t
+
+        def merged(words):
+            return words[0].rearrange("p n t -> p (n t)")
+
+        xo_sc_win = zeroed_plane("xo_sc_win", M, "slot_c")
+        w2_sc_raw = zeroed_plane("w2_sc_raw", R)
+        w2_sc_rows = tile("w2_sc_rows", [4, QUADS, R], U8, "slot_d")
+        nc.sync.dma_start(
+            out=w2_sc_rows[:].bitcast(I32),
+            in_=w2_scales[0].rearrange("(q i) n -> i q n", i=4).bitcast(I32),
+        )
+        l2 = load_list("l2", offs2)
+        xo_win = tile("xo_win", [P, M], U16, "slot_a")
+        load_words(xo_win, xo_words[0])
+        load_scale_rows(xo_sc_win, xo_scales, nc.scalar)
+        w2_raw = tile("w2_raw", [P, R], U32, "slot_b")
+        load_words(w2_raw, merged(w2_words))
+        l4 = load_list("l4", offs4)
+        pv = [zeroed_board("pv0"), zeroed_board("pv1")]
+
+        xt_sc_win = zeroed_plane("xt_sc_win", T)
+        w_sc_raw = zeroed_plane("w_sc_raw", R)
+        vs_sc_win = zeroed_plane("vs_sc_win", S)
+        xt_win = tile("xt_win", [P, T], U32)
+        load_words(xt_win, merged(xt_words))
+        w_raw = tile("w_raw", [P, 2 * R], U8)
+        load_words(w_raw, w_words[0])
+        l1 = load_list("l1", offs)
+        load_scale_rows(xt_sc_win, xt_scales)
+        load_scale_rows(w_sc_raw, w_scales)
+        l3 = load_list("l3", offs3)
+        vs_win = tile("vs_win", [P, S], U32)
+        load_words(vs_win, merged(vs_words))
+        load_scale_rows(vs_sc_win, vs_scales)
+        l6 = load_list("l6", offs6)
+        l5 = load_list("l5", offs5)
+        sa_t = tile("sa_t", [P, PACK], F32)
+        nc.sync.dma_start(out=sa_t[:], in_=sa.rearrange("(p t) o -> p (t o)", t=PACK))
+
+        for q in range(QUADS):
+            nc.vector.tensor_copy(
+                out=w2_sc_raw[32 * q : 32 * q + 4, :].bitcast(I32), in_=w2_sc_rows[:, q, :].bitcast(I32)
+            )
+        xo_g = tile("xo_g", [P, J], U16)
+        xo_sc_g = tile("xo_sc_g", [P, J], U8)
+        w2_d = tile("w2_d", [P, PACK, P], U32)
+        w2_sc_d = tile("w2_sc_d", [P, PACK, P], U8)
+        w2_raw_v = w2_raw[:].rearrange("p (m t) -> p t m", t=PACK)
+        w2_sc_v = w2_sc_raw[:].rearrange("p (m t) -> p t m", t=PACK)
+
+        gather(xo_g, xo_win, l2, 0, HALF)
+        nc.vector.tensor_copy(out=w2_sc_d[:, 0, :], in_=w2_sc_v[:, 0, :])
+        gather(xo_sc_g, xo_sc_win, l2, 0, HALF)
+        nc.scalar.copy(out=w2_d[:, 0, :], in_=w2_raw_v[:, 0, :])
+
+        def product_b(t, lo, hi):
+            acc = psum.tile([P, J], F32, name="acc")
+            nc.tensor.matmul_mx(
+                out=acc[:, lo:hi],
+                lhsT=w2_d[:, t, :].bitcast(FP8X4), lhsT_scale=w2_sc_d[:, t, :],
+                rhs=xo_g[:, lo:hi].bitcast(FP4X4), rhs_scale=xo_sc_g[:, lo:hi],
+                start=True, stop=True,
+            )
+            vals = tile("b_%d_%d" % (t, lo), [P, hi - lo], F32)
+            nc.vector.tensor_copy(out=vals[:], in_=acc[:, lo:hi])
+            nc.scalar.activation(out=pv[t][:].indirect(l4[:, lo // 16 : hi // 16]), in_=vals[:], func=COPY)
+
+        product_b(0, 0, HALF)
+        gather(xo_sc_g, xo_sc_win, l2, HALF, J)
+        gather(xo_g, xo_win, l2, HALF, J)
+        nc.scalar.copy(
+            out=w2_d[:, 1:PACK, :].rearrange("p t (c i) -> p c t i", i=4),
+            in_=w2_raw_v[:, 1:PACK, :].rearrange("p t (c i) -> p c t i", i=4),
+        )
+        product_b(0, HALF, J)
+        nc.vector.tensor_copy(out=w2_sc_d[:, 1:PACK, :], in_=w2_sc_v[:, 1:PACK, :])
+        product_b(1, 0, J)
+        pv.append(zeroed_board("pv2", "slot_c"))
+        product_b(2, 0, J)
+        pv.append(zeroed_board("pv3", "slot_d"))
+        product_b(3, 0, J)
+
+        xt_g = tile("xt_g", [P, J], U32)
+        xt_sc_g = tile("xt_sc_g", [P, J], U8)
+        w_d = tile("w_d", [P, PACK, 2 * P], U8)
+        w_sc_d = tile("w_sc_d", [P, PACK, P], U8)
+        gather(xt_g, xt_win, l1, 0, J)
+        nc.vector.tensor_copy(
+            out=w_d[:].rearrange("p t (m b) -> p m t b", b=2),
+            in_=w_raw[:].rearrange("p (m t b) -> p m t b", t=PACK, b=2),
+        )
+        gather(xt_sc_g, xt_sc_win, l1, 0, J)
+        nc.vector.tensor_copy(out=w_sc_d[:], in_=w_sc_raw[:].rearrange("p (m t) -> p t m", t=PACK))
+        pw = [zeroed_board("pw0", "slot_a"), zeroed_board("pw1", "slot_b")]
+
+        a_vals = []
+        for t in range(PACK):
+            acc = psum.tile([P, J], F32, name="acc")
+            nc.tensor.matmul_mx(
+                out=acc[:],
+                lhsT=w_d[:, t, :].bitcast(FP4X4), lhsT_scale=w_sc_d[:, t, :],
+                rhs=xt_g[:].bitcast(FP8X4), rhs_scale=xt_sc_g[:],
+                start=True, stop=True,
+            )
+            vals = tile("a_%d" % t, [P, J], F32, "slot_e" if t == PACK - 1 else None)
+            nc.vector.tensor_copy(out=vals[:], in_=acc[:])
+            a_vals.append(vals)
+
+        vs_g = tile("vs_g", [P, N], U32)
+        vs_sc_g = tile("vs_sc_g", [P, N], U8)
+        gather(vs_g, vs_win, l6, 0, N)
+        gather(vs_sc_g, vs_sc_win, l6, 0, N)
+
+        pg = []
+        for t in range(PACK):
+            board = pw[t % 2]
+            nc.scalar.activation(out=board[:].indirect(l3[:]), in_=a_vals[t][:], func=COPY)
+            left = tile("pg_%d" % t, [P, C], F32)
+            nc.vector.tensor_copy(out=left[:, 0:1], in_=board[:, 0:1])
+            nc.vector.tensor_tensor(out=left[:, 1:C], in0=board[:, 1:C], in1=pv[t][:, 0 : C - 1], op=SUB)
+            pg.append(left)
+
+        planes = tile("planes", [P, 2, PACK, HALF], BF16, "slot_e")
+        for h in range(2):
+            for t in range(PACK):
+                nc.scalar.activation(
+                    out=planes[:, h, t, :],
+                    in_=pg[t][:].indirect(l5[:, h * HALF // 16 : (h + 1) * HALF // 16]),
+                    func=COPY, scale=sa_t[:, t : t + 1],
+                )
+        out_v = out.rearrange("(u p) o -> p u o", p=P)
+        for h in range(2):
+            woven = tile("woven_%d" % h, [P, HALF, PACK], BF16)
+            nc.vector.tensor_copy(
+                out=woven[:].rearrange("p (c i) t -> p c t i", i=4),
+                in_=planes[:, h, :, :].rearrange("p t (c i) -> p c t i", i=4),
+            )
+            hq = tile("hq_%d" % h, [P, HALF], U32)
+            hq_sc = tile("hq_sc_%d" % h, [P, HALF], U8)
+            nc.vector.quantize_mx(
+                out=hq[:].bitcast(FP8X4), scales=hq_sc[:], in_=woven[:].rearrange("p o t -> p (o t)")
+            )
+            cols = slice(h * HALF, (h + 1) * HALF)
+
+            def last_product(dst, u):
+                nc.tensor.matmul_mx(
+                    out=dst,
+                    lhsT=vs_g[:, u * P : (u + 1) * P].bitcast(FP8X4), lhsT_scale=vs_sc_g[:, u * P : (u + 1) * P],
+                    rhs=hq[:].bitcast(FP8X4), rhs_scale=hq_sc[:],
+                    start=True, stop=True,
+                )
+
+            if h == 0:
+                acc = psum.tile([P, J], F32, name="acc")
+                for u in range(2):
+                    last_product(acc[:, u * HALF : (u + 1) * HALF], u)
+                res = tile("res_0", [P, 2, HALF], F32)
+                nc.scalar.copy(out=res[:].rearrange("p u o -> p (u o)"), in_=acc[:])
+                nc.sync.dma_start(out=out_v[:, :, cols], in_=res[:])
+            else:
+                for u in range(2):
+                    acc = psum.tile([P, J], F32, name="acc")
+                    last_product(acc[:, 0:HALF], u)
+                    res = tile("res_1_%d" % u, [P, HALF], F32)
+                    if u == 0:
+                        nc.vector.tensor_copy(out=res[:], in_=acc[:, 0:HALF])
+                        nc.sync.dma_start(out=out_v[:, u, cols], in_=res[:])
+                    else:
+                        nc.scalar.copy(out=res[:], in_=acc[:, 0:HALF])
+                        nc.scalar.dma_start(out=out_v[:, u, cols], in_=res[:])

@@ -31,6 +31,7 @@ def tile_picked_tokens_plain_two_lagged_store_plain_kernel(
     with ExitStack() as ctx:
         lists = ctx.enter_context(tc.tile_pool(name="lists", bufs=1))
         sb = ctx.enter_context(tc.tile_pool(name="sb", bufs=1))
+        shared = ctx.enter_context(tc.tile_pool(name="shared", bufs=1))
         psum = ctx.enter_context(tc.psum_pool(name="psum", bufs=8))
 
         def tile(name, shape, dtype, tag=None):
@@ -67,9 +68,10 @@ def tile_picked_tokens_plain_two_lagged_store_plain_kernel(
         def merged(words):
             return words[0].rearrange("p n t -> p (n t)")
 
-        xo_sc_win = zeroed_plane("xo_sc_win", M, "slot_c")
+        xo_sc_win = shared.tile([P, M], U8, name="xo_sc_win", align_bytes=ALIGN, offset=0)
+        nc.vector.memset(xo_sc_win[:].bitcast(I32), 0)
         w2_sc_raw = zeroed_plane("w2_sc_raw", R)
-        w2_sc_rows = tile("w2_sc_rows", [4, QUADS, R], U8, "slot_d")
+        w2_sc_rows = tile("w2_sc_rows", [4, QUADS, R], U8)
         nc.sync.dma_start(
             out=w2_sc_rows[:].bitcast(I32),
             in_=w2_scales[0].rearrange("(q i) n -> i q n", i=4).bitcast(I32),
@@ -81,11 +83,12 @@ def tile_picked_tokens_plain_two_lagged_store_plain_kernel(
         w2_raw = tile("w2_raw", [P, R], U32, "slot_b")
         load_words(w2_raw, merged(w2_words))
         l4 = load_list("l4", offs4)
-        pv = [zeroed_board("pv0"), zeroed_board("pv1")]
+        pv = [zeroed_board("pv0")]
 
         xt_sc_win = zeroed_plane("xt_sc_win", T)
         w_sc_raw = zeroed_plane("w_sc_raw", R)
         vs_sc_win = zeroed_plane("vs_sc_win", S)
+        pv.extend(zeroed_board("pv%d" % t) for t in range(1, PACK))
         xt_win = tile("xt_win", [P, T], U32)
         load_words(xt_win, merged(xt_words))
         w_raw = tile("w_raw", [P, 2 * R], U8)
@@ -93,7 +96,6 @@ def tile_picked_tokens_plain_two_lagged_store_plain_kernel(
         l1 = load_list("l1", offs)
         load_scale_rows(xt_sc_win, xt_scales)
         load_scale_rows(w_sc_raw, w_scales)
-        l3 = load_list("l3", offs3)
         vs_win = tile("vs_win", [P, S], U32)
         load_words(vs_win, merged(vs_words))
         load_scale_rows(vs_sc_win, vs_scales)
@@ -101,49 +103,57 @@ def tile_picked_tokens_plain_two_lagged_store_plain_kernel(
         l5 = load_list("l5", offs5)
         sa_t = tile("sa_t", [P, PACK], F32)
         nc.sync.dma_start(out=sa_t[:], in_=sa.rearrange("(p t) o -> p (t o)", t=PACK))
+        l3 = load_list("l3", offs3)
 
         for q in range(QUADS):
             nc.vector.tensor_copy(
                 out=w2_sc_raw[32 * q : 32 * q + 4, :].bitcast(I32), in_=w2_sc_rows[:, q, :].bitcast(I32)
             )
-        xo_g = tile("xo_g", [P, J], U16)
         xo_sc_g = tile("xo_sc_g", [P, J], U8)
         w2_d = tile("w2_d", [P, PACK, P], U32)
-        w2_sc_d = tile("w2_sc_d", [P, PACK, P], U8)
+        w2_sc_first = tile("w2_sc_first", [P, P], U8)
         w2_raw_v = w2_raw[:].rearrange("p (m t) -> p t m", t=PACK)
         w2_sc_v = w2_sc_raw[:].rearrange("p (m t) -> p t m", t=PACK)
 
-        gather(xo_g, xo_win, l2, 0, HALF)
-        nc.vector.tensor_copy(out=w2_sc_d[:, 0, :], in_=w2_sc_v[:, 0, :])
-        gather(xo_sc_g, xo_sc_win, l2, 0, HALF)
+        xo_g = [tile("xo_g0", [P, HALF], U16)]
+        nc.vector.tensor_copy(out=w2_sc_first[:], in_=w2_sc_v[:, 0, :])
+        nc.vector.tensor_copy(out=xo_g[0][:], in_=xo_win[:].indirect(l2[:, 0 : HALF // 16]))
+        gather(xo_sc_g, xo_sc_win, l2, 0, J)
         nc.scalar.copy(out=w2_d[:, 0, :], in_=w2_raw_v[:, 0, :])
 
-        def product_b(t, lo, hi):
-            acc = psum.tile([P, J], F32, name="acc")
+        def pass_b(acc, t, h, scale_plane):
+            cols = slice(h * HALF, (h + 1) * HALF)
             nc.tensor.matmul_mx(
-                out=acc[:, lo:hi],
-                lhsT=w2_d[:, t, :].bitcast(FP8X4), lhsT_scale=w2_sc_d[:, t, :],
-                rhs=xo_g[:, lo:hi].bitcast(FP4X4), rhs_scale=xo_sc_g[:, lo:hi],
+                out=acc[:, cols],
+                lhsT=w2_d[:, t, :].bitcast(FP8X4), lhsT_scale=scale_plane,
+                rhs=xo_g[h][:].bitcast(FP4X4), rhs_scale=xo_sc_g[:, cols],
                 start=True, stop=True,
             )
+
+        def put_b(acc, t, lo, hi, copy):
             vals = tile("b_%d_%d" % (t, lo), [P, hi - lo], F32)
-            nc.vector.tensor_copy(out=vals[:], in_=acc[:, lo:hi])
+            copy(out=vals[:], in_=acc[:, lo:hi])
             nc.scalar.activation(out=pv[t][:].indirect(l4[:, lo // 16 : hi // 16]), in_=vals[:], func=COPY)
 
-        product_b(0, 0, HALF)
-        gather(xo_sc_g, xo_sc_win, l2, HALF, J)
-        gather(xo_g, xo_win, l2, HALF, J)
+        acc = psum.tile([P, J], F32, name="acc")
+        pass_b(acc, 0, 0, w2_sc_first[:])
         nc.scalar.copy(
             out=w2_d[:, 1:PACK, :].rearrange("p t (c i) -> p c t i", i=4),
             in_=w2_raw_v[:, 1:PACK, :].rearrange("p t (c i) -> p c t i", i=4),
         )
-        product_b(0, HALF, J)
-        nc.vector.tensor_copy(out=w2_sc_d[:, 1:PACK, :], in_=w2_sc_v[:, 1:PACK, :])
-        product_b(1, 0, J)
-        pv.append(zeroed_board("pv2", "slot_c"))
-        product_b(2, 0, J)
-        pv.append(zeroed_board("pv3", "slot_d"))
-        product_b(3, 0, J)
+        put_b(acc, 0, 0, HALF, nc.scalar.copy)
+        xo_g.append(shared.tile([P, HALF], U16, name="xo_g1", align_bytes=ALIGN, offset=512))
+        nc.vector.tensor_copy(out=xo_g[1][:], in_=xo_win[:].indirect(l2[:, HALF // 16 : J // 16]))
+        acc = psum.tile([P, J], F32, name="acc")
+        pass_b(acc, 0, 1, w2_sc_first[:])
+        put_b(acc, 0, HALF, J, nc.vector.tensor_copy)
+        w2_sc_rest = shared.tile([P, PACK - 1, P], U8, name="w2_sc_rest", align_bytes=ALIGN, offset=0)
+        nc.vector.tensor_copy(out=w2_sc_rest[:], in_=w2_sc_v[:, 1:PACK, :])
+        for t in range(1, PACK):
+            acc = psum.tile([P, J], F32, name="acc")
+            for h in range(2):
+                pass_b(acc, t, h, w2_sc_rest[:, t - 1, :])
+            put_b(acc, t, 0, J, nc.vector.tensor_copy)
 
         xt_g = tile("xt_g", [P, J], U32)
         xt_sc_g = tile("xt_sc_g", [P, J], U8)
@@ -185,11 +195,14 @@ def tile_picked_tokens_plain_two_lagged_store_plain_kernel(
             nc.vector.tensor_tensor(out=left[:, 1:C], in0=board[:, 1:C], in1=pv[t][:, 0 : C - 1], op=SUB)
             pg.append(left)
 
-        planes = tile("planes", [P, 2, PACK, HALF], BF16, "slot_e")
+        planes = [
+            tile("planes0", [P, PACK, HALF], BF16, "slot_e"),
+            tile("planes1", [P, PACK, HALF], BF16, "pv%d" % (PACK - 1)),
+        ]
         for h in range(2):
             for t in range(PACK):
                 nc.scalar.activation(
-                    out=planes[:, h, t, :],
+                    out=planes[h][:, t, :],
                     in_=pg[t][:].indirect(l5[:, h * HALF // 16 : (h + 1) * HALF // 16]),
                     func=COPY, scale=sa_t[:, t : t + 1],
                 )
@@ -198,7 +211,7 @@ def tile_picked_tokens_plain_two_lagged_store_plain_kernel(
             woven = tile("woven_%d" % h, [P, HALF, PACK], BF16)
             nc.vector.tensor_copy(
                 out=woven[:].rearrange("p (c i) t -> p c t i", i=4),
-                in_=planes[:, h, :, :].rearrange("p t (c i) -> p c t i", i=4),
+                in_=planes[h][:].rearrange("p t (c i) -> p c t i", i=4),
             )
             hq = tile("hq_%d" % h, [P, HALF], U32)
             hq_sc = tile("hq_sc_%d" % h, [P, HALF], U8)

@@ -100,10 +100,10 @@ def tile_picked_tokens_plain_two_lagged_store_plain_kernel(
         load_words(vs_win, merged(vs_words))
         load_scale_rows(vs_sc_win, vs_scales)
         l6 = load_list("l6", offs6)
+        l3 = load_list("l3", offs3)
         l5 = load_list("l5", offs5)
         sa_t = tile("sa_t", [P, PACK], F32)
         nc.sync.dma_start(out=sa_t[:], in_=sa.rearrange("(p t) o -> p (t o)", t=PACK))
-        l3 = load_list("l3", offs3)
 
         for q in range(QUADS):
             nc.vector.tensor_copy(
@@ -142,14 +142,18 @@ def tile_picked_tokens_plain_two_lagged_store_plain_kernel(
             in_=w2_raw_v[:, 1:PACK, :].rearrange("p t (c i) -> p c t i", i=4),
         )
         put_b(acc, 0, 0, HALF, nc.scalar.copy)
-        xo_g.append(shared.tile([P, HALF], U16, name="xo_g1", align_bytes=ALIGN, offset=512))
-        nc.vector.tensor_copy(out=xo_g[1][:], in_=xo_win[:].indirect(l2[:, HALF // 16 : J // 16]))
-        acc = psum.tile([P, J], F32, name="acc")
-        pass_b(acc, 0, 1, w2_sc_first[:])
-        put_b(acc, 0, HALF, J, nc.vector.tensor_copy)
         w2_sc_rest = shared.tile([P, PACK - 1, P], U8, name="w2_sc_rest", align_bytes=ALIGN, offset=0)
         nc.vector.tensor_copy(out=w2_sc_rest[:], in_=w2_sc_v[:, 1:PACK, :])
-        for t in range(1, PACK):
+        acc = psum.tile([P, J], F32, name="acc")
+        pass_b(acc, 1, 0, w2_sc_rest[:, 0, :])
+        put_b(acc, 1, 0, HALF, nc.vector.tensor_copy)
+        xo_g.append(shared.tile([P, HALF], U16, name="xo_g1", align_bytes=ALIGN, offset=512))
+        nc.vector.tensor_copy(out=xo_g[1][:], in_=xo_win[:].indirect(l2[:, HALF // 16 : J // 16]))
+        for t in range(2):
+            acc = psum.tile([P, J], F32, name="acc")
+            pass_b(acc, t, 1, w2_sc_rest[:, 0, :] if t else w2_sc_first[:])
+            put_b(acc, t, HALF, J, nc.vector.tensor_copy)
+        for t in range(2, PACK):
             acc = psum.tile([P, J], F32, name="acc")
             for h in range(2):
                 pass_b(acc, t, h, w2_sc_rest[:, t - 1, :])
@@ -157,29 +161,31 @@ def tile_picked_tokens_plain_two_lagged_store_plain_kernel(
 
         xt_g = tile("xt_g", [P, J], U32)
         xt_sc_g = tile("xt_sc_g", [P, J], U8)
-        w_d = tile("w_d", [P, PACK, 2 * P], U8)
-        w_sc_d = tile("w_sc_d", [P, PACK, P], U8)
+        w_raw_v = w_raw[:].rearrange("p (m t b) -> p m t b", t=PACK, b=2)
+        w_sc_v = w_sc_raw[:].rearrange("p (m t) -> p t m", t=PACK)
         gather(xt_g, xt_win, l1, 0, J)
-        nc.vector.tensor_copy(
-            out=w_d[:].rearrange("p t (m b) -> p m t b", b=2),
-            in_=w_raw[:].rearrange("p (m t b) -> p m t b", t=PACK, b=2),
-        )
         gather(xt_sc_g, xt_sc_win, l1, 0, J)
-        nc.vector.tensor_copy(out=w_sc_d[:], in_=w_sc_raw[:].rearrange("p (m t) -> p t m", t=PACK))
-        pw = [zeroed_board("pw0", "slot_a"), zeroed_board("pw1", "slot_b")]
 
         a_vals = []
-        for t in range(PACK):
-            acc = psum.tile([P, J], F32, name="acc")
-            nc.tensor.matmul_mx(
-                out=acc[:],
-                lhsT=w_d[:, t, :].bitcast(FP4X4), lhsT_scale=w_sc_d[:, t, :],
-                rhs=xt_g[:].bitcast(FP8X4), rhs_scale=xt_sc_g[:],
-                start=True, stop=True,
-            )
-            vals = tile("a_%d" % t, [P, J], F32, "slot_e" if t == PACK - 1 else None)
-            nc.vector.tensor_copy(out=vals[:], in_=acc[:])
-            a_vals.append(vals)
+        for pair in range(2):
+            ts = slice(2 * pair, 2 * pair + 2)
+            w_d = tile("w_d%d" % pair, [P, 2, 2 * P], U8, "w_d")
+            w_sc_d = tile("w_sc_d%d" % pair, [P, 2, P], U8, "w_sc_d")
+            nc.vector.tensor_copy(out=w_d[:].rearrange("p t (m b) -> p m t b", b=2), in_=w_raw_v[:, :, ts, :])
+            nc.vector.tensor_copy(out=w_sc_d[:], in_=w_sc_v[:, ts, :])
+            for i in range(2):
+                t = 2 * pair + i
+                acc = psum.tile([P, J], F32, name="acc")
+                nc.tensor.matmul_mx(
+                    out=acc[:],
+                    lhsT=w_d[:, i, :].bitcast(FP4X4), lhsT_scale=w_sc_d[:, i, :],
+                    rhs=xt_g[:].bitcast(FP8X4), rhs_scale=xt_sc_g[:],
+                    start=True, stop=True,
+                )
+                vals = tile("a_%d" % t, [P, J], F32, "slot_e" if t == PACK - 1 else None)
+                nc.vector.tensor_copy(out=vals[:], in_=acc[:])
+                a_vals.append(vals)
+        pw = [zeroed_board("pw0", "xt_win"), zeroed_board("pw1", "xt_sc_win")]
 
         vs_g = tile("vs_g", [P, N], U32)
         vs_sc_g = tile("vs_sc_g", [P, N], U8)

from contextlib import ExitStack

import concourse.mybir as mybir

K, J, R, T, Z, M, C, O, N, S = 512, 256, 512, 1024, 512, 1024, 512, 256, 256, 1024
FLOPS = 2 * K * R * J + 2 * Z * R * J + 2 * R * N * O

F32 = mybir.dt.float32
BF16 = mybir.dt.bfloat16
I32 = mybir.dt.int32
U32 = mybir.dt.uint32
U16 = mybir.dt.uint16
U8 = mybir.dt.uint8
FP8X4 = mybir.dt.float8_e4m3fn_x4
FP4X4 = mybir.dt.float4_e2m1fn_x4
COPY = mybir.ActivationFunctionType.Copy
SUB = mybir.AluOpType.subtract

P = 128
PACK = 4
QUADS = 4
HALF = 128
ALIGN = 64


def tile_picked_tokens_plain_two_lagged_store_plain_kernel(
    tc, xt_words, xt_scales, w_words, w_scales, xo_words, xo_scales, w2_words, w2_scales, sa,
    vs_words, vs_scales, offs, offs2, offs3, offs4, offs5, offs6, out,
):
    nc = tc.nc
    with ExitStack() as ctx:
        lists = ctx.enter_context(tc.tile_pool(name="lists", bufs=1))
        sb = ctx.enter_context(tc.tile_pool(name="sb", bufs=1))
        shared = ctx.enter_context(tc.tile_pool(name="shared", bufs=1))
        psum = ctx.enter_context(tc.psum_pool(name="psum", bufs=8))

        def tile(name, shape, dtype, tag=None):
            return sb.tile(shape, dtype, name=name, tag=tag or name, align_bytes=ALIGN)

        def load_list(name, src):
            t = lists.tile([P, J // 16], U16, name=name)
            nc.sync.dma_start(t[:], src)
            return t

        def load_words(dst, src):
            nc.sync.dma_start(out=dst[:].bitcast(I32), in_=src.bitcast(I32))

        def zeroed_plane(name, width, tag=None):
            t = tile(name, [P, width], U8, tag)
            nc.vector.memset(t[:].bitcast(I32), 0)
            return t

        def load_scale_rows(plane, scales, queue=None):
            for q in range(QUADS):
                (queue or nc.sync).dma_start(
                    out=plane[32 * q : 32 * q + 4, :].bitcast(I32),
                    in_=scales[0][4 * q : 4 * q + 4, :].bitcast(I32),
                )

        def gather(dst, window, offsets, lo, hi):
            nc.vector.tensor_copy(out=dst[:, lo:hi], in_=window[:].indirect(offsets[:, lo // 16 : hi // 16]))

        def zeroed_board(name, tag=None):
            t = tile(name, [P, C], F32, tag)
            nc.vector.memset(t[:], 0.0)
            return t

        def merged(words):
            return words[0].rearrange("p n t -> p (n t)")

        xo_sc_win = shared.tile([P, M], U8, name="xo_sc_win", align_bytes=ALIGN, offset=0)
        nc.vector.memset(xo_sc_win[:].bitcast(I32), 0)
        w2_sc_raw = zeroed_plane("w2_sc_raw", R)
        w2_sc_rows = tile("w2_sc_rows", [4, QUADS, R], U8)
        nc.sync.dma_start(
            out=w2_sc_rows[:].bitcast(I32),
            in_=w2_scales[0].rearrange("(q i) n -> i q n", i=4).bitcast(I32),
        )
        l2 = load_list("l2", offs2)
        xo_win = tile("xo_win", [P, M], U16, "slot_a")
        load_words(xo_win, xo_words[0])
        load_scale_rows(xo_sc_win, xo_scales, nc.scalar)
        w2_raw = tile("w2_raw", [P, R], U32, "slot_b")
        load_words(w2_raw, merged(w2_words))
        l4 = load_list("l4", offs4)
        pv = [zeroed_board("pv0")]

        xt_sc_win = zeroed_plane("xt_sc_win", T)
        w_sc_raw = zeroed_plane("w_sc_raw", R)
        vs_sc_win = zeroed_plane("vs_sc_win", S)
        pv.extend(zeroed_board("pv%d" % t) for t in range(1, PACK))
        xt_win = tile("xt_win", [P, T], U32)
        load_words(xt_win, merged(xt_words))
        w_raw = tile("w_raw", [P, 2 * R], U8)
        load_words(w_raw, w_words[0])
        l1 = load_list("l1", offs)
        load_scale_rows(xt_sc_win, xt_scales)
        load_scale_rows(w_sc_raw, w_scales)
        vs_win = tile("vs_win", [P, S], U32)
        load_words(vs_win, merged(vs_words))
        load_scale_rows(vs_sc_win, vs_scales)
        l6 = load_list("l6", offs6)
        l3 = load_list("l3", offs3)
        l5 = load_list("l5", offs5)
        sa_t = tile("sa_t", [P, PACK], F32)
        nc.sync.dma_start(out=sa_t[:], in_=sa.rearrange("(p t) o -> p (t o)", t=PACK))

        for q in range(QUADS):
            nc.vector.tensor_copy(
                out=w2_sc_raw[32 * q : 32 * q + 4, :].bitcast(I32), in_=w2_sc_rows[:, q, :].bitcast(I32)
            )
        xo_sc_g = tile("xo_sc_g", [P, J], U8)
        w2_d = tile("w2_d", [P, PACK, P], U32)
        w2_sc_first = tile("w2_sc_first", [P, P], U8)
        w2_raw_v = w2_raw[:].rearrange("p (m t) -> p t m", t=PACK)
        w2_sc_v = w2_sc_raw[:].rearrange("p (m t) -> p t m", t=PACK)

        xo_g = [tile("xo_g0", [P, HALF], U16)]
        nc.vector.tensor_copy(out=w2_sc_first[:], in_=w2_sc_v[:, 0, :])
        nc.vector.tensor_copy(out=xo_g[0][:], in_=xo_win[:].indirect(l2[:, 0 : HALF // 16]))
        gather(xo_sc_g, xo_sc_win, l2, 0, J)
        nc.scalar.copy(out=w2_d[:, 0, :], in_=w2_raw_v[:, 0, :])

        def pass_b(acc, t, h, scale_plane):
            cols = slice(h * HALF, (h + 1) * HALF)
            nc.tensor.matmul_mx(
                out=acc[:, cols],
                lhsT=w2_d[:, t, :].bitcast(FP8X4), lhsT_scale=scale_plane,
                rhs=xo_g[h][:].bitcast(FP4X4), rhs_scale=xo_sc_g[:, cols],
                start=True, stop=True,
            )

        def put_b(acc, t, lo, hi, copy):
            vals = tile("b_%d_%d" % (t, lo), [P, hi - lo], F32)
            copy(out=vals[:], in_=acc[:, lo:hi])
            nc.scalar.activation(out=pv[t][:].indirect(l4[:, lo // 16 : hi // 16]), in_=vals[:], func=COPY)

        acc = psum.tile([P, J], F32, name="acc")
        pass_b(acc, 0, 0, w2_sc_first[:])
        nc.scalar.copy(
            out=w2_d[:, 1:PACK, :].rearrange("p t (c i) -> p c t i", i=4),
            in_=w2_raw_v[:, 1:PACK, :].rearrange("p t (c i) -> p c t i", i=4),
        )
        put_b(acc, 0, 0, HALF, nc.scalar.copy)
        w2_sc_rest = shared.tile([P, PACK - 1, P], U8, name="w2_sc_rest", align_bytes=ALIGN, offset=0)
        nc.vector.tensor_copy(out=w2_sc_rest[:], in_=w2_sc_v[:, 1:PACK, :])
        acc = psum.tile([P, J], F32, name="acc")
        pass_b(acc, 1, 0, w2_sc_rest[:, 0, :])
        put_b(acc, 1, 0, HALF, nc.vector.tensor_copy)
        xo_g.append(shared.tile([P, HALF], U16, name="xo_g1", align_bytes=ALIGN, offset=512))
        nc.vector.tensor_copy(out=xo_g[1][:], in_=xo_win[:].indirect(l2[:, HALF // 16 : J // 16]))
        for t in range(2):
            acc = psum.tile([P, J], F32, name="acc")
            pass_b(acc, t, 1, w2_sc_rest[:, 0, :] if t else w2_sc_first[:])
            put_b(acc, t, HALF, J, nc.vector.tensor_copy)
        for t in range(2, PACK):
            acc = psum.tile([P, J], F32, name="acc")
            for h in range(2):
                pass_b(acc, t, h, w2_sc_rest[:, t - 1, :])
            put_b(acc, t, 0, J, nc.vector.tensor_copy)

        xt_g = tile("xt_g", [P, J], U32)
        xt_sc_g = tile("xt_sc_g", [P, J], U8)
        w_raw_v = w_raw[:].rearrange("p (m t b) -> p m t b", t=PACK, b=2)
        w_sc_v = w_sc_raw[:].rearrange("p (m t) -> p t m", t=PACK)
        gather(xt_g, xt_win, l1, 0, J)
        gather(xt_sc_g, xt_sc_win, l1, 0, J)

        a_vals = []
        for pair in range(2):
            ts = slice(2 * pair, 2 * pair + 2)
            w_d = tile("w_d%d" % pair, [P, 2, 2 * P], U8, "w_d")
            w_sc_d = tile("w_sc_d%d" % pair, [P, 2, P], U8, "w_sc_d")
            nc.vector.tensor_copy(out=w_d[:].rearrange("p t (m b) -> p m t b", b=2), in_=w_raw_v[:, :, ts, :])
            nc.vector.tensor_copy(out=w_sc_d[:], in_=w_sc_v[:, ts, :])
            for i in range(2):
                t = 2 * pair + i
                acc = psum.tile([P, J], F32, name="acc")
                nc.tensor.matmul_mx(
                    out=acc[:],
                    lhsT=w_d[:, i, :].bitcast(FP4X4), lhsT_scale=w_sc_d[:, i, :],
                    rhs=xt_g[:].bitcast(FP8X4), rhs_scale=xt_sc_g[:],
                    start=True, stop=True,
                )
                vals = tile("a_%d" % t, [P, J], F32, "slot_e" if t == PACK - 1 else None)
                nc.vector.tensor_copy(out=vals[:], in_=acc[:])
                a_vals.append(vals)
        pw = [zeroed_board("pw0", "xt_win"), zeroed_board("pw1", "xt_sc_win")]

        vs_g = tile("vs_g", [P, N], U32)
        vs_sc_g = tile("vs_sc_g", [P, N], U8)
        gather(vs_g, vs_win, l6, 0, N)
        gather(vs_sc_g, vs_sc_win, l6, 0, N)

        pg = []
        for t in range(PACK):
            board = pw[t % 2]
            nc.scalar.activation(out=board[:].indirect(l3[:]), in_=a_vals[t][:], func=COPY)
            left = tile("pg_%d" % t, [P, C], F32)
            nc.vector.tensor_copy(out=left[:, 0:1], in_=board[:, 0:1])
            nc.vector.tensor_tensor(out=left[:, 1:C], in0=board[:, 1:C], in1=pv[t][:, 0 : C - 1], op=SUB)
            pg.append(left)

        planes = [
            tile("planes0", [P, PACK, HALF], BF16, "slot_e"),
            tile("planes1", [P, PACK, HALF], BF16, "pv%d" % (PACK - 1)),
        ]
        for h in range(2):
            for t in range(PACK):
                nc.scalar.activation(
                    out=planes[h][:, t, :],
                    in_=pg[t][:].indirect(l5[:, h * HALF // 16 : (h + 1) * HALF // 16]),
                    func=COPY, scale=sa_t[:, t : t + 1],
                )
        out_v = out.rearrange("(u p) o -> p u o", p=P)
        for h in range(2):
            woven = tile("woven_%d" % h, [P, HALF, PACK], BF16)
            nc.vector.tensor_copy(
                out=woven[:].rearrange("p (c i) t -> p c t i", i=4),
                in_=planes[h][:].rearrange("p t (c i) -> p c t i", i=4),
            )
            hq = tile("hq_%d" % h, [P, HALF], U32)
            hq_sc = tile("hq_sc_%d" % h, [P, HALF], U8)
            nc.vector.quantize_mx(
                out=hq[:].bitcast(FP8X4), scales=hq_sc[:], in_=woven[:].rearrange("p o t -> p (o t)")
            )
            cols = slice(h * HALF, (h + 1) * HALF)

            def last_product(dst, u):
                nc.tensor.matmul_mx(
                    out=dst,
                    lhsT=vs_g[:, u * P : (u + 1) * P].bitcast(FP8X4), lhsT_scale=vs_sc_g[:, u * P : (u + 1) * P],
                    rhs=hq[:].bitcast(FP8X4), rhs_scale=hq_sc[:],
                    start=True, stop=True,
                )

            if h == 0:
                acc = psum.tile([P, J], F32, name="acc")
                for u in range(2):
                    last_product(acc[:, u * HALF : (u + 1) * HALF], u)
                res = tile("res_0", [P, 2, HALF], F32)
                nc.scalar.copy(out=res[:].rearrange("p u o -> p (u o)"), in_=acc[:])
                nc.sync.dma_start(out=out_v[:, :, cols], in_=res[:])
            else:
                for u in range(2):
                    acc = psum.tile([P, J], F32, name="acc")
                    last_product(acc[:, 0:HALF], u)
                    res = tile("res_1_%d" % u, [P, HALF], F32)
                    if u == 0:
                        nc.vector.tensor_copy(out=res[:], in_=acc[:, 0:HALF])
                        nc.sync.dma_start(out=out_v[:, u, cols], in_=res[:])
                    else:
                        nc.scalar.copy(out=res[:], in_=acc[:, 0:HALF])
                        nc.scalar.dma_start(out=out_v[:, u, cols], in_=res[:])
